import numpy as np
import ml_dtypes


def mxq(x, axis, fmt="e4m3"):
    dtype, down = {"e4m3": (ml_dtypes.float8_e4m3fn, 7), "e5m2": (ml_dtypes.float8_e5m2, 14)}[fmt]
    v = np.moveaxis(np.asarray(x, np.float32).astype(ml_dtypes.bfloat16).astype(np.float64), axis, -1)
    blocks = v.reshape(v.shape[:-1] + (-1, 32))
    amax = np.abs(blocks).max(-1, keepdims=True)
    byte = np.maximum(np.where(amax > 0, np.frexp(amax)[1] - 1 + 127, 0) - down, 1)
    scale = np.exp2(byte - 127.0)
    codes = (blocks / scale).astype(np.float32).astype(dtype).astype(np.float64)
    return np.moveaxis((codes * scale).reshape(v.shape), -1, axis)


WIDE = False


def mx_kscale(k):
    if not WIDE:
        return np.ones(k)
    levels = np.array([10, -10, 5, -5, 0])
    if k % 512:
        return np.exp2(np.random.permutation(np.resize(levels, k // 32))).repeat(32)
    a = np.empty((k // 512, 16))
    for p in range(k // 512):
        a[p, :8] = np.random.permutation(np.resize(levels, 8))
        for g in range(8):
            far = levels[np.abs(levels - a[p, g]) >= 10]
            a[p, g + 8] = far[np.random.randint(len(far))]
    return np.exp2(a.ravel()).repeat(32)


def f64(x):
    return np.asarray(x).astype(np.float64)


def striped(idx):
    return np.tile(np.asarray(idx).reshape(-1, 16).T, (8, 1)).astype(np.uint16)


def unstriped(offs):
    return offs[:16].T.reshape(-1).astype(np.int64)


E2M1 = np.array([0.0, 0.5, 1.0, 1.5, 2.0, 3.0, 4.0, 6.0, -0.0, -0.5, -1.0, -1.5, -2.0, -3.0, -4.0, -6.0])


def pack_weight(w, fmt):
    k, n = w.shape
    w = f64(np.asarray(w, np.float32).astype(ml_dtypes.bfloat16)).reshape(k // 32, 32, n)
    amax = np.abs(w).max(1)
    if fmt == "e4m3":
        byte = np.frexp(amax)[1] - 1 + 127 - 7
    else:
        mant, ex = np.frexp(amax / 6.0)
        byte = np.where(mant > 0.5, ex, ex - 1) + 127
    byte = np.clip(np.where(amax > 0, byte, 1), 1, 254)
    scaled = (w * np.exp2(127.0 - byte)[:, None, :]).reshape(k, n).astype(np.float32)
    by_word = np.ascontiguousarray(scaled.reshape(k // 512, 128, 4, n).transpose(0, 1, 3, 2))
    if fmt == "e4m3":
        words = by_word.astype(ml_dtypes.float8_e4m3fn).view(np.uint8)
    else:
        c = by_word.astype(ml_dtypes.float4_e2m1fn).view(np.uint8) & 0xF
        words = (c[..., 0::2] | (c[..., 1::2] << 4)).reshape(k // 512, 128, 2 * n)
    return np.ascontiguousarray(words), np.ascontiguousarray(byte.astype(np.uint8).reshape(k // 512, 16, n))


def unpack_weight(words, scales, fmt):
    g, _, n = scales.shape
    words = np.ascontiguousarray(words).reshape(g, 128, n, -1)
    if fmt == "e4m3":
        vals = words.view(ml_dtypes.float8_e4m3fn).astype(np.float64)
    else:
        nib = np.empty((g, 128, n, 4), np.uint8)
        nib[..., 0::2] = words & 0xF
        nib[..., 1::2] = words >> 4
        vals = E2M1[nib]
    vals = vals * np.repeat(np.exp2(scales.astype(np.float64) - 127.0), 8, axis=1)[..., None]
    return vals.transpose(0, 1, 3, 2).reshape(g * 512, n)


def bf(x):
    return np.asarray(x, np.float32).astype(ml_dtypes.bfloat16)


def planes(Y):
    r, m = Y.shape
    b = f64(bf(Y)).reshape(r // 32, 32, m)
    amax = np.abs(b).max(1)
    byte = np.clip(np.where(amax > 0, np.frexp(amax)[1] - 1 + 127 - 7, 1), 1, 254)
    codes = (b * np.exp2(127.0 - byte)[:, None, :]).reshape(r, m).astype(np.float32).astype(ml_dtypes.float8_e4m3fn).view(np.uint8)
    words = codes.reshape(r // 512, 128, 4, m).transpose(0, 1, 3, 2)
    return np.ascontiguousarray(words), np.ascontiguousarray(byte.astype(np.uint8).reshape(r // 512, 16, m))


D, T, I, Q, X = 512, 4096, 1024, 512, 64


def setup_inputs():
    n = np.random.standard_normal
    idx = np.random.permutation(T)[:I]
    fd = mx_kscale(D)
    vocp = pack_weight(n((D, T)) / fd[:, None], "e4m3")
    return {
        "hid": (n((D, Q)) * 1.0 / np.sqrt(D) * fd[:, None]).astype(np.float32),
        "voc_words": vocp[0],
        "voc_scales": vocp[1],
        "pd": (np.random.uniform(0.05, 0.2, (Q, 1))).astype(np.float32),
        "offs": striped(idx),
    }


def reference(hid, voc_words, voc_scales, pd, offs):
    idx = unstriped(offs)
    vocu = unpack_weight(voc_words, voc_scales, "e4m3")
    hidq = mxq(f64(hid), 0, "e4m3")
    vocidxg = vocu[:, idx]
    a = hidq.T @ vocidxg
    p = np.exp(a - np.max(a, axis=1, keepdims=True))
    w = p * f64(pd) / np.sum(p, axis=1, keepdims=True)
    wt = w.T
    y = wt.reshape(I, X, Q // X).sum(axis=2) * 512.0
    words, scales = planes(y)
    return y, words, scales

@@ -1,0 +1,182 @@
+from contextlib import ExitStack
+
+import concourse.mybir as mybir
+from concourse.masks import make_identity
+
+D, T, I, Q, X = 512, 4096, 1024, 512, 64
+FLOPS = 2 * D * Q * I
+
+F32 = mybir.dt.float32
+BF16 = mybir.dt.bfloat16
+I32 = mybir.dt.int32
+U32 = mybir.dt.uint32
+U16 = mybir.dt.uint16
+U8 = mybir.dt.uint8
+FP8X4 = mybir.dt.float8_e4m3fn_x4
+ALU = mybir.AluOpType
+ACT = mybir.ActivationFunctionType
+AXIS_X = mybir.AxisListType.X
+
+P = 128
+PACK = 4
+BLOCKS = Q // P
+HALVES = 2
+HALF = I // HALVES
+OUT_SCALE = 512.0
+SPLIT = 108
+POOL_BLOCKS = 2
+
+
+def tile_attend_ragmarginal_pl_kernel(tc, hid, voc_words, voc_scales, pd, offs, out_0, out_1, out_2):
+    nc = tc.nc
+    with ExitStack() as ctx:
+        lists = ctx.enter_context(tc.tile_pool(name="lists", bufs=1))
+        sb = ctx.enter_context(tc.tile_pool(name="sb", bufs=1))
+        psum = ctx.enter_context(tc.psum_pool(name="psum", bufs=1))
+
+        offsets = lists.tile([P, I // 16], U16, name="offsets")
+        nc.sync.dma_start(offsets[:], offs)
+
+        scale_rows = sb.tile([P, T], U8, name="scale_rows", align_bytes=64)
+        nc.sync.dma_start(out=scale_rows[16:32, :].bitcast(I32), in_=voc_scales[0].bitcast(I32))
+        for lo, hi in ((0, 16), (32, 64), (64, P)):
+            nc.vector.memset(scale_rows[lo:hi, :].bitcast(I32), 0)
+
+        words = sb.tile([P, T], I32, name="words", align_bytes=64)
+        nc.sync.dma_start(out=words[:], in_=voc_words[0].rearrange("p n t -> p (n t)").bitcast(I32))
+        hid_rows = hid.rearrange("(k t) q -> k t q", t=PACK)
+        hid_half = []
+        for h in range(2):
+            part = sb.tile([P, PACK, Q // 2], F32, name="hid%d" % h)
+            nc.sync.dma_start(out=part[:], in_=hid_rows[:, :, h * (Q // 2):(h + 1) * (Q // 2)])
+            hid_half.append(part)
+
+        pd_raw = sb.tile([P, BLOCKS], F32, name="pd_raw")
+        nc.scalar.dma_start(out=pd_raw[:], in_=pd.rearrange("(p r) o -> p (r o)", r=BLOCKS))
+
+        plane = sb.tile([P, I], U8, name="plane", align_bytes=64)
+        nc.gpsimd.memset(plane[:].bitcast(I32), 0)
+        ident = sb.tile([P, P], F32, name="ident")
+        make_identity(nc, ident[:])
+
+        pd_out = sb.tile([P, BLOCKS], F32, name="pd_out")
+        nc.scalar.activation(out=pd_out[:], in_=pd_raw[:], func=ACT.Copy, scale=OUT_SCALE)
+
+        picked_scales = sb.tile([P, I], U8, name="picked_scales", align_bytes=64)
+        nc.vector.tensor_copy(picked_scales[:], scale_rows[:].indirect(offsets[:]))
+        for quad in range(4):
+            nc.scalar.dma_start(
+                out=plane[32 * quad:32 * quad + 4, :].bitcast(I32),
+                in_=picked_scales[16 + 4 * quad:20 + 4 * quad, :].bitcast(I32),
+            )
+
+        picked = []
+        for g in range(HALVES):
+            part = sb.tile([P, HALF], U32, name="picked%d" % g, align_bytes=64)
+            cols = slice(g * (HALF // 16), (g + 1) * (HALF // 16))
+            nc.vector.tensor_copy(part[:], words[:].bitcast(U32).indirect(offsets[:, cols]))
+            picked.append(part)
+
+        dealt = sb.tile([P, BLOCKS, P, PACK], BF16, name="dealt", align_bytes=64)
+
+        def deal(copy, lo, hi):
+            h = lo // (P // 2)
+            a, b = lo - h * (P // 2), hi - h * (P // 2)
+            src = hid_half[h][:, :, BLOCKS * a:BLOCKS * b].rearrange("k t (p r) -> k p t r", r=BLOCKS)
+            copy(out=dealt[:, :, lo:hi, :].rearrange("k r p t -> k p t r"), in_=src)
+
+        deal(nc.scalar.copy, 0, P // 2)
+        deal(nc.vector.tensor_copy, P // 2, SPLIT)
+        deal(nc.scalar.copy, SPLIT, P)
+
+        scores = []
+        for r in range(BLOCKS):
+            codes = sb.tile([P, P], U32, name="hid_codes%d" % r, align_bytes=64)
+            scales = sb.tile([P, P], U8, name="hid_scales%d" % r, align_bytes=64)
+            nc.vector.quantize_mx(
+                out=codes[:].bitcast(FP8X4), scales=scales[:],
+                in_=dealt[:, r, :, :].rearrange("k p t -> k (p t)"),
+            )
+            acc = psum.tile([P, I], F32, name="scores%d" % r, tag="banks%d" % r)
+            for g in range(HALVES):
+                cols = slice(g * HALF, (g + 1) * HALF)
+                nc.tensor.matmul_mx(
+                    out=acc[:, cols], lhsT=codes[:].bitcast(FP8X4), lhsT_scale=scales[:],
+                    rhs=picked[g][:].bitcast(FP8X4), rhs_scale=plane[:, cols], start=True, stop=True,
+                )
+            scores.append(acc)
+
+        probs, sums, lifts = [], [], []
+        for r in range(BLOCKS):
+            neg_max = sb.tile([P, HALVES], F32, name="neg_max%d" % r)
+            prob = sb.tile([P, HALVES, PACK, P], F32, name="prob%d" % r)
+            part_sums = sb.tile([P, HALVES], F32, name="part_sums%d" % r)
+            for g in range(HALVES):
+                bank = scores[r][:, g * HALF:(g + 1) * HALF]
+                nc.vector.tensor_reduce(out=neg_max[:, g:g + 1], in_=bank, axis=AXIS_X, op=ALU.max, negate=True)
+                nc.scalar.activation(
+                    out=prob[:, g], in_=bank.rearrange("q (m t) -> q t m", t=PACK),
+                    func=ACT.Exp, bias=neg_max[:, g:g + 1], scale=1.0, accum_out=part_sums[:, g:g + 1],
+                )
+            neg_row_max = sb.tile([P, 1], F32, name="neg_row_max%d" % r)
+            nc.vector.tensor_reduce(out=neg_row_max[:], in_=neg_max[:], axis=AXIS_X, op=ALU.min)
+            lift = sb.tile([P, HALVES], F32, name="lift%d" % r)
+            nc.scalar.activation(out=lift[:], in_=neg_max[:], func=ACT.Exp, bias=neg_row_max[:], scale=-1.0)
+            probs.append(prob)
+            sums.append(part_sums)
+            lifts.append(lift)
+
+        turned = psum.tile([P, HALVES, PACK, P], F32, name="turned", tag="banks0")
+        for r in range(BLOCKS):
+            lift_pd = sb.tile([P, HALVES], F32, name="lift_pd%d" % r)
+            nc.gpsimd.tensor_scalar(
+                out=lift_pd[:], in0=lifts[r][:], scalar1=pd_out[:, r:r + 1], scalar2=0.0, op0=ALU.mult, op1=ALU.add,
+            )
+            terms = sb.tile([P, HALVES], F32, name="terms%d" % r)
+            total = sb.tile([P, 1], F32, name="total%d" % r)
+            nc.vector.scalar_tensor_tensor(
+                out=terms[:], in0=sums[r][:], scalar=1.0, in1=lifts[r][:], op0=ALU.mult, op1=ALU.mult, accum_out=total[:],
+            )
+            inv = sb.tile([P, 1], F32, name="inv%d" % r)
+            nc.vector.reciprocal(out=inv[:], in_=total[:])
+            weight = sb.tile([P, HALVES, PACK, P], F32, name="weight%d" % r)
+            engine = nc.gpsimd if r < POOL_BLOCKS else nc.vector
+            for g in range(HALVES):
+                engine.tensor_scalar(
+                    out=weight[:, g].rearrange("q t m -> q (t m)"), in0=probs[r][:, g].rearrange("q t m -> q (t m)"),
+                    scalar1=inv[:], scalar2=lift_pd[:, g:g + 1], op0=ALU.mult, op1=ALU.mult,
+                )
+                for t in range(PACK):
+                    nc.tensor.matmul(
+                        out=turned[:, g, t, :], lhsT=weight[:, g, t, :], rhs=ident[:], is_transpose=True,
+                        start=(r == 0 and t == 0), stop=(r == BLOCKS - 1 and t == PACK - 1),
+                    )
+
+        rounded = sb.tile([P, HALVES, X, PACK], BF16, name="rounded", align_bytes=64)
+        out_rows = out_0.rearrange("(g p t) x -> g p t x", g=HALVES, t=PACK)
+        for g in range(HALVES):
+            result = sb.tile([P, PACK, X], F32, name="result%d" % g)
+            nc.vector.tensor_reduce(
+                out=result[:].rearrange("p t x -> p (t x)"),
+                in_=turned[:, g].rearrange("p t (x s) -> p (t x) s", s=2), axis=AXIS_X, op=ALU.add,
+            )
+            nc.sync.dma_start(out=out_rows[g], in_=result[:])
+            copy = nc.scalar.copy if g == 0 else nc.vector.tensor_copy
+            copy(out=rounded[:, g], in_=result[:].rearrange("p t x -> p x t"))
+
+        out_codes = sb.tile([P, HALVES * X], I32, name="out_codes", align_bytes=64)
+        out_scales = sb.tile([P, HALVES * X], U8, name="out_scales", align_bytes=64)
+        nc.vector.quantize_mx(
+            out=out_codes[:].bitcast(FP8X4), scales=out_scales[:],
+            in_=rounded[:].rearrange("p g x t -> p (g x t)"),
+        )
+        nc.sync.dma_start(
+            out=out_1.rearrange("g p x t -> p g (x t)").bitcast(I32),
+            in_=out_codes[:].rearrange("p (g x) -> p g x", g=HALVES),
+        )
+        for quad in range(4):
+            queue = nc.scalar if quad % 2 == 0 else nc.sync
+            queue.dma_start(
+                out=out_2[:, 4 * quad:4 * quad + 4, :].rearrange("g r x -> r g x").bitcast(I32),
+                in_=out_scales[32 * quad:32 * quad + 4, :].bitcast(I32).rearrange("r (g x) -> r g x", g=HALVES),
+            )

@@ -23,7 +23,7 @@ BLOCKS = Q // P
 HALVES = 2
 HALF = I // HALVES
 OUT_SCALE = 512.0
-SPLIT = 108
+SPLIT = 54
 POOL_BLOCKS = 2
 
 
@@ -51,8 +51,10 @@ def tile_attend_ragmarginal_pl_kernel(tc, hid, voc_words, voc_scales, pd, offs, 
             nc.sync.dma_start(out=part[:], in_=hid_rows[:, :, h * (Q // 2):(h + 1) * (Q // 2)])
             hid_half.append(part)
 
-        pd_raw = sb.tile([P, BLOCKS], F32, name="pd_raw")
-        nc.scalar.dma_start(out=pd_raw[:], in_=pd.rearrange("(p r) o -> p (r o)", r=BLOCKS))
+        pd_raw = sb.tile([P, 8], F32, name="pd_raw")
+        pd_rows = pd.rearrange("(x j) o -> x (j o)", j=8)
+        for s in range(2):
+            nc.scalar.dma_start(out=pd_raw[s:P:2, 0:7], in_=pd_rows[:, s:s + 7])
 
         plane = sb.tile([P, I], U8, name="plane", align_bytes=64)
         nc.gpsimd.memset(plane[:].bitcast(I32), 0)
@@ -60,7 +62,7 @@ def tile_attend_ragmarginal_pl_kernel(tc, hid, voc_words, voc_scales, pd, offs, 
         make_identity(nc, ident[:])
 
         pd_out = sb.tile([P, BLOCKS], F32, name="pd_out")
-        nc.scalar.activation(out=pd_out[:], in_=pd_raw[:], func=ACT.Copy, scale=OUT_SCALE)
+        nc.scalar.activation(out=pd_out[:], in_=pd_raw[:, 0:7:2], func=ACT.Copy, scale=OUT_SCALE)
 
         picked_scales = sb.tile([P, I], U8, name="picked_scales", align_bytes=64)
         nc.vector.tensor_copy(picked_scales[:], scale_rows[:].indirect(offsets[:]))
@@ -80,14 +82,14 @@ def tile_attend_ragmarginal_pl_kernel(tc, hid, voc_words, voc_scales, pd, offs, 
         dealt = sb.tile([P, BLOCKS, P, PACK], BF16, name="dealt", align_bytes=64)
 
         def deal(copy, lo, hi):
-            h = lo // (P // 2)
-            a, b = lo - h * (P // 2), hi - h * (P // 2)
-            src = hid_half[h][:, :, BLOCKS * a:BLOCKS * b].rearrange("k t (p r) -> k p t r", r=BLOCKS)
-            copy(out=dealt[:, :, lo:hi, :].rearrange("k r p t -> k p t r"), in_=src)
+            h = lo // (X // 2)
+            a, b = lo - h * (X // 2), hi - h * (X // 2)
+            src = hid_half[h][:, :, 8 * a:8 * b].rearrange("k t (x r s) -> k x r t s", r=BLOCKS, s=2)
+            copy(out=dealt[:, :, 2 * lo:2 * hi, :].rearrange("k r (x s) t -> k x r t s", s=2), in_=src)
 
-        deal(nc.scalar.copy, 0, P // 2)
-        deal(nc.vector.tensor_copy, P // 2, SPLIT)
-        deal(nc.scalar.copy, SPLIT, P)
+        deal(nc.scalar.copy, 0, X // 2)
+        deal(nc.vector.tensor_copy, X // 2, SPLIT)
+        deal(nc.scalar.copy, SPLIT, X)
 
         scores = []
         for r in range(BLOCKS):
@@ -97,72 +99,100 @@ def tile_attend_ragmarginal_pl_kernel(tc, hid, voc_words, voc_scales, pd, offs, 
                 out=codes[:].bitcast(FP8X4), scales=scales[:],
                 in_=dealt[:, r, :, :].rearrange("k p t -> k (p t)"),
             )
-            acc = psum.tile([P, I], F32, name="scores%d" % r, tag="banks%d" % r)
+            banks = []
             for g in range(HALVES):
                 cols = slice(g * HALF, (g + 1) * HALF)
+                acc = psum.tile([P, HALF], F32, name="scores%d_%d" % (r, g), tag="bank%d" % (HALVES * r + g))
+                banks.append(acc)
                 nc.tensor.matmul_mx(
-                    out=acc[:, cols], lhsT=codes[:].bitcast(FP8X4), lhsT_scale=scales[:],
+                    out=acc[:], lhsT=codes[:].bitcast(FP8X4), lhsT_scale=scales[:],
                     rhs=picked[g][:].bitcast(FP8X4), rhs_scale=plane[:, cols], start=True, stop=True,
                 )
-            scores.append(acc)
+            scores.append(banks)
 
-        probs, sums, lifts = [], [], []
-        for r in range(BLOCKS):
-            neg_max = sb.tile([P, HALVES], F32, name="neg_max%d" % r)
-            prob = sb.tile([P, HALVES, PACK, P], F32, name="prob%d" % r)
-            part_sums = sb.tile([P, HALVES], F32, name="part_sums%d" % r)
-            for g in range(HALVES):
-                bank = scores[r][:, g * HALF:(g + 1) * HALF]
-                nc.vector.tensor_reduce(out=neg_max[:, g:g + 1], in_=bank, axis=AXIS_X, op=ALU.max, negate=True)
-                nc.scalar.activation(
-                    out=prob[:, g], in_=bank.rearrange("q (m t) -> q t m", t=PACK),
-                    func=ACT.Exp, bias=neg_max[:, g:g + 1], scale=1.0, accum_out=part_sums[:, g:g + 1],
-                )
-            neg_row_max = sb.tile([P, 1], F32, name="neg_row_max%d" % r)
-            nc.vector.tensor_reduce(out=neg_row_max[:], in_=neg_max[:], axis=AXIS_X, op=ALU.min)
-            lift = sb.tile([P, HALVES], F32, name="lift%d" % r)
-            nc.scalar.activation(out=lift[:], in_=neg_max[:], func=ACT.Exp, bias=neg_row_max[:], scale=-1.0)
-            probs.append(prob)
-            sums.append(part_sums)
-            lifts.append(lift)
+        turned = []
+        negated = sb.tile([P, HALF], BF16, name="negated")
 
-        turned = psum.tile([P, HALVES, PACK, P], F32, name="turned", tag="banks0")
-        for r in range(BLOCKS):
-            lift_pd = sb.tile([P, HALVES], F32, name="lift_pd%d" % r)
-            nc.gpsimd.tensor_scalar(
-                out=lift_pd[:], in0=lifts[r][:], scalar1=pd_out[:, r:r + 1], scalar2=0.0, op0=ALU.mult, op1=ALU.add,
+        def first_half(r):
+            neg_max = sb.tile([P, 1], F32, name="neg_max%d" % r)
+            prob = sb.tile([P, PACK, P], F32, name="prob%d_0" % r)
+            part_sum = sb.tile([P, 1], F32, name="part_sum%d_0" % r)
+            bank = scores[r][0][:]
+            nc.vector.tensor_reduce(out=neg_max[:], in_=bank, axis=AXIS_X, op=ALU.max, negate=True)
+            nc.scalar.activation(
+                out=prob[:], in_=bank.rearrange("q (m t) -> q t m", t=PACK),
+                func=ACT.Exp, bias=neg_max[:], scale=1.0, accum_out=part_sum[:],
             )
-            terms = sb.tile([P, HALVES], F32, name="terms%d" % r)
+            return neg_max, prob, part_sum
+
+        def second_half(r, neg_max):
+            neg_row_max = sb.tile([P, 1], F32, name="neg_row_max%d" % r)
+            prob = sb.tile([P, PACK, P], F32, name="prob%d_1" % r)
+            part_sum = sb.tile([P, 1], F32, name="part_sum%d_1" % r)
+            bank = scores[r][1][:]
+            nc.vector.tensor_scalar(
+                out=negated[:], in0=bank, scalar1=-1.0, scalar2=neg_max[:], op0=ALU.mult, op1=ALU.min,
+                accum_out=neg_row_max[:],
+            )
+            lift = sb.tile([P, 1], F32, name="lift%d" % r)
+            nc.scalar.activation(out=lift[:], in_=neg_max[:], func=ACT.Exp, bias=neg_row_max[:], scale=-1.0)
+            nc.scalar.activation(
+                out=prob[:], in_=bank.rearrange("q (m t) -> q t m", t=PACK),
+                func=ACT.Exp, bias=neg_row_max[:], scale=1.0, accum_out=part_sum[:],
+            )
+            return lift, prob, part_sum
+
+        def weigh(r, lift, probs, sums):
+            if r == 0:
+                turned.extend([psum.tile([P, PACK, P], F32, name="turned%d" % g, tag="bank%d" % g) for g in range(HALVES)])
+            lift_pd = sb.tile([P, 1], F32, name="lift_pd%d" % r)
+            nc.gpsimd.tensor_scalar(
+                out=lift_pd[:], in0=lift[:], scalar1=pd_out[:, r:r + 1], scalar2=0.0, op0=ALU.mult, op1=ALU.add,
+            )
+            term = sb.tile([P, 1], F32, name="term%d" % r)
             total = sb.tile([P, 1], F32, name="total%d" % r)
-            nc.vector.scalar_tensor_tensor(
-                out=terms[:], in0=sums[r][:], scalar=1.0, in1=lifts[r][:], op0=ALU.mult, op1=ALU.mult, accum_out=total[:],
+            nc.vector.tensor_scalar(
+                out=term[:], in0=sums[0][:], scalar1=lift[:], scalar2=sums[1][:], op0=ALU.mult, op1=ALU.add,
+                accum_out=total[:],
             )
             inv = sb.tile([P, 1], F32, name="inv%d" % r)
             nc.vector.reciprocal(out=inv[:], in_=total[:])
-            weight = sb.tile([P, HALVES, PACK, P], F32, name="weight%d" % r)
             engine = nc.gpsimd if r < POOL_BLOCKS else nc.vector
-            for g in range(HALVES):
+            for g in (1, 0):
+                weight = sb.tile([P, PACK, P], F32, name="weight%d_%d" % (r, g))
                 engine.tensor_scalar(
-                    out=weight[:, g].rearrange("q t m -> q (t m)"), in0=probs[r][:, g].rearrange("q t m -> q (t m)"),
-                    scalar1=inv[:], scalar2=lift_pd[:, g:g + 1], op0=ALU.mult, op1=ALU.mult,
+                    out=weight[:].rearrange("q t m -> q (t m)"), in0=probs[g][:].rearrange("q t m -> q (t m)"),
+                    scalar1=inv[:], scalar2=lift_pd[:] if g == 0 else pd_out[:, r:r + 1], op0=ALU.mult, op1=ALU.mult,
                 )
                 for t in range(PACK):
                     nc.tensor.matmul(
-                        out=turned[:, g, t, :], lhsT=weight[:, g, t, :], rhs=ident[:], is_transpose=True,
+                        out=turned[g][:, t, :], lhsT=weight[:, t, :], rhs=ident[:], is_transpose=True,
                         start=(r == 0 and t == 0), stop=(r == BLOCKS - 1 and t == PACK - 1),
                     )
 
+        pending = None
+        for r in range(BLOCKS):
+            neg_max, prob0, sum0 = first_half(r)
+            if pending is not None:
+                weigh(*pending)
+            lift, prob1, sum1 = second_half(r, neg_max)
+            pending = (r, lift, (prob0, prob1), (sum0, sum1))
+        weigh(*pending)
+
         rounded = sb.tile([P, HALVES, X, PACK], BF16, name="rounded", align_bytes=64)
         out_rows = out_0.rearrange("(g p t) x -> g p t x", g=HALVES, t=PACK)
-        for g in range(HALVES):
+        for g in (1, 0):
             result = sb.tile([P, PACK, X], F32, name="result%d" % g)
             nc.vector.tensor_reduce(
                 out=result[:].rearrange("p t x -> p (t x)"),
-                in_=turned[:, g].rearrange("p t (x s) -> p (t x) s", s=2), axis=AXIS_X, op=ALU.add,
+                in_=turned[g][:].rearrange("p t (x s) -> p (t x) s", s=2), axis=AXIS_X, op=ALU.add,
             )
             nc.sync.dma_start(out=out_rows[g], in_=result[:])
-            copy = nc.scalar.copy if g == 0 else nc.vector.tensor_copy
-            copy(out=rounded[:, g], in_=result[:].rearrange("p t x -> p x t"))
+            copy = nc.scalar.copy if g == 1 else nc.vector.tensor_copy
+            copy(
+                out=rounded[:, g].rearrange("p (c i) t -> p c t i", i=4),
+                in_=result[:].rearrange("p t (c i) -> p c t i", i=4),
+            )
 
         out_codes = sb.tile([P, HALVES * X], I32, name="out_codes", align_bytes=64)
         out_scales = sb.tile([P, HALVES * X], U8, name="out_scales", align_bytes=64)

@@ -23,8 +23,9 @@ BLOCKS = Q // P
 HALVES = 2
 HALF = I // HALVES
 OUT_SCALE = 512.0
-SPLIT = 54
-POOL_BLOCKS = 2
+POOL_UNITS = ((0, 1), (0, 0), (1, 1))
+SCALAR_UNITS = ((2, 1),)
+ORDER = (1, 0)
 
 
 def tile_attend_ragmarginal_pl_kernel(tc, hid, voc_words, voc_scales, pd, offs, out_0, out_1, out_2):
@@ -63,6 +64,7 @@ def tile_attend_ragmarginal_pl_kernel(tc, hid, voc_words, voc_scales, pd, offs, 
 
         pd_out = sb.tile([P, BLOCKS], F32, name="pd_out")
         nc.scalar.activation(out=pd_out[:], in_=pd_raw[:, 0:7:2], func=ACT.Copy, scale=OUT_SCALE)
+        held = {}
 
         picked_scales = sb.tile([P, I], U8, name="picked_scales", align_bytes=64)
         nc.vector.tensor_copy(picked_scales[:], scale_rows[:].indirect(offsets[:]))
@@ -79,45 +81,48 @@ def tile_attend_ragmarginal_pl_kernel(tc, hid, voc_words, voc_scales, pd, offs, 
             nc.vector.tensor_copy(part[:], words[:].bitcast(U32).indirect(offsets[:, cols]))
             picked.append(part)
 
-        dealt = sb.tile([P, BLOCKS, P, PACK], BF16, name="dealt", align_bytes=64)
+        dealt = {first: sb.tile([P, 2, P, PACK], BF16, name="dealt%d" % first, align_bytes=64) for first in (0, 2)}
 
-        def deal(copy, lo, hi):
-            h = lo // (X // 2)
-            a, b = lo - h * (X // 2), hi - h * (X // 2)
-            src = hid_half[h][:, :, 8 * a:8 * b].rearrange("k t (x r s) -> k x r t s", r=BLOCKS, s=2)
-            copy(out=dealt[:, :, 2 * lo:2 * hi, :].rearrange("k r (x s) t -> k x r t s", s=2), in_=src)
+        def deal(copy, h, first):
+            src = hid_half[h][:].rearrange("k t (x r s) -> k x r t s", r=BLOCKS, s=2)
+            dst = dealt[first][:, :, h * X:(h + 1) * X, :].rearrange("k r (x s) t -> k x r t s", s=2)
+            copy(out=dst, in_=src[:, :, first:first + 2])
 
-        deal(nc.scalar.copy, 0, X // 2)
-        deal(nc.vector.tensor_copy, X // 2, SPLIT)
-        deal(nc.scalar.copy, SPLIT, X)
+        deal(nc.scalar.copy, 0, 0)
+        deal(nc.scalar.copy, 0, 2)
+        deal(nc.vector.tensor_copy, 1, 0)
+        deal(nc.scalar.copy, 1, 2)
 
-        scores = []
-        for r in range(BLOCKS):
-            codes = sb.tile([P, P], U32, name="hid_codes%d" % r, align_bytes=64)
-            scales = sb.tile([P, P], U8, name="hid_scales%d" % r, align_bytes=64)
+        quantised = []
+        for first, count in ((0, 1), (1, 1), (2, 2)):
+            codes = sb.tile([P, count * P], U32, name="hid_codes%d" % first, align_bytes=64)
+            scales = sb.tile([P, count * P], U8, name="hid_scales%d" % first, align_bytes=64)
             nc.vector.quantize_mx(
                 out=codes[:].bitcast(FP8X4), scales=scales[:],
-                in_=dealt[:, r, :, :].rearrange("k p t -> k (p t)"),
+                in_=dealt[first - first % 2][:, first % 2:first % 2 + count, :, :].rearrange("k r p t -> k (r p t)"),
             )
-            banks = []
-            for g in range(HALVES):
-                cols = slice(g * HALF, (g + 1) * HALF)
-                acc = psum.tile([P, HALF], F32, name="scores%d_%d" % (r, g), tag="bank%d" % (HALVES * r + g))
-                banks.append(acc)
-                nc.tensor.matmul_mx(
-                    out=acc[:], lhsT=codes[:].bitcast(FP8X4), lhsT_scale=scales[:],
-                    rhs=picked[g][:].bitcast(FP8X4), rhs_scale=plane[:, cols], start=True, stop=True,
-                )
-            scores.append(banks)
+            for j in range(count):
+                quantised.append((codes[:, j * P:(j + 1) * P], scales[:, j * P:(j + 1) * P]))
 
-        turned = []
+        scores = {}
+
+        def score(r, g):
+            codes, scales = quantised[r]
+            acc = psum.tile([P, HALF], F32, name="scores%d_%d" % (r, g), tag="score_bank%d" % (len(scores) % 4))
+            nc.tensor.matmul_mx(
+                out=acc[:], lhsT=codes.bitcast(FP8X4), lhsT_scale=scales,
+                rhs=picked[g][:].bitcast(FP8X4), rhs_scale=plane[:, g * HALF:(g + 1) * HALF], start=True, stop=True,
+            )
+            scores[r, g] = acc
+
+        turned = {}
         negated = sb.tile([P, HALF], BF16, name="negated")
 
         def first_half(r):
             neg_max = sb.tile([P, 1], F32, name="neg_max%d" % r)
             prob = sb.tile([P, PACK, P], F32, name="prob%d_0" % r)
             part_sum = sb.tile([P, 1], F32, name="part_sum%d_0" % r)
-            bank = scores[r][0][:]
+            bank = scores[r, 0][:]
             nc.vector.tensor_reduce(out=neg_max[:], in_=bank, axis=AXIS_X, op=ALU.max, negate=True)
             nc.scalar.activation(
                 out=prob[:], in_=bank.rearrange("q (m t) -> q t m", t=PACK),
@@ -125,11 +130,11 @@ def tile_attend_ragmarginal_pl_kernel(tc, hid, voc_words, voc_scales, pd, offs, 
             )
             return neg_max, prob, part_sum
 
-        def second_half(r, neg_max):
-            neg_row_max = sb.tile([P, 1], F32, name="neg_row_max%d" % r)
+        def second_half(r, neg_max, first_sum):
+            neg_row_max = sb.tile([P, 1], F32, name="neg_row_max%d" % r, tag="row_stat%d" % (r % 2))
             prob = sb.tile([P, PACK, P], F32, name="prob%d_1" % r)
             part_sum = sb.tile([P, 1], F32, name="part_sum%d_1" % r)
-            bank = scores[r][1][:]
+            bank = scores[r, 1][:]
             nc.vector.tensor_scalar(
                 out=negated[:], in0=bank, scalar1=-1.0, scalar2=neg_max[:], op0=ALU.mult, op1=ALU.min,
                 accum_out=neg_row_max[:],
@@ -140,55 +145,97 @@ def tile_attend_ragmarginal_pl_kernel(tc, hid, voc_words, voc_scales, pd, offs, 
                 out=prob[:], in_=bank.rearrange("q (m t) -> q t m", t=PACK),
                 func=ACT.Exp, bias=neg_row_max[:], scale=1.0, accum_out=part_sum[:],
             )
-            return lift, prob, part_sum
+            lift_pd = None
+            if (r, 1) not in SCALAR_UNITS:
+                lift_pd = sb.tile([P, 1], F32, name="lift_pd%d" % r)
+                if (r, 0) in POOL_UNITS:
+                    nc.gpsimd.tensor_scalar(
+                        out=lift_pd[:], in0=lift[:], scalar1=pd_out[:, r:r + 1], scalar2=0.0, op0=ALU.mult, op1=ALU.add,
+                    )
+                else:
+                    nc.scalar.activation(out=lift_pd[:], in_=lift[:], func=ACT.Copy, scale=pd_out[:, r:r + 1])
+            total = sb.tile([P, 1], F32, name="total%d" % r, tag="row_stat%d" % (r % 2))
+            nc.scalar.activation(out=total[:], in_=first_sum[:], func=ACT.Identity, scale=lift[:], bias=part_sum[:])
+            return lift, lift_pd, prob, total
 
-        def weigh(r, lift, probs, sums):
+        def weigh(r, lift, lift_pd, probs, total):
             if r == 0:
-                turned.extend([psum.tile([P, PACK, P], F32, name="turned%d" % g, tag="bank%d" % g) for g in range(HALVES)])
-            lift_pd = sb.tile([P, 1], F32, name="lift_pd%d" % r)
-            nc.gpsimd.tensor_scalar(
-                out=lift_pd[:], in0=lift[:], scalar1=pd_out[:, r:r + 1], scalar2=0.0, op0=ALU.mult, op1=ALU.add,
-            )
-            term = sb.tile([P, 1], F32, name="term%d" % r)
-            total = sb.tile([P, 1], F32, name="total%d" % r)
-            nc.vector.tensor_scalar(
-                out=term[:], in0=sums[0][:], scalar1=lift[:], scalar2=sums[1][:], op0=ALU.mult, op1=ALU.add,
-                accum_out=total[:],
-            )
+                for g in ORDER:
+                    for h in range(2):
+                        turned[g, h] = psum.tile([P, 2, P], F32, name="turned%d_%d" % (g, h), tag="result_bank%d" % len(turned))
             inv = sb.tile([P, 1], F32, name="inv%d" % r)
             nc.vector.reciprocal(out=inv[:], in_=total[:])
-            engine = nc.gpsimd if r < POOL_BLOCKS else nc.vector
-            for g in (1, 0):
-                weight = sb.tile([P, PACK, P], F32, name="weight%d_%d" % (r, g))
-                engine.tensor_scalar(
-                    out=weight[:].rearrange("q t m -> q (t m)"), in0=probs[g][:].rearrange("q t m -> q (t m)"),
-                    scalar1=inv[:], scalar2=lift_pd[:] if g == 0 else pd_out[:, r:r + 1], op0=ALU.mult, op1=ALU.mult,
-                )
-                for t in range(PACK):
-                    nc.tensor.matmul(
-                        out=turned[g][:, t, :], lhsT=weight[:, t, :], rhs=ident[:], is_transpose=True,
-                        start=(r == 0 and t == 0), stop=(r == BLOCKS - 1 and t == PACK - 1),
-                    )
+            if (r, 1) in SCALAR_UNITS:
+                joint = sb.tile([P, 1], F32, name="joint%d" % r)
+                nc.vector.tensor_scalar(out=joint[:], in0=inv[:], scalar1=pd_out[:, r:r + 1], scalar2=None, op0=ALU.mult)
+            if (r - 1, 1) in SCALAR_UNITS:
+                joint = sb.tile([P, 1], F32, name="joint%d" % r)
+                nc.scalar.activation(out=joint[:], in_=inv[:], func=ACT.Copy, scale=pd_out[:, r:r + 1])
+            step = 2 if r == BLOCKS - 1 else PACK
+            for g in (ORDER[::-1] if r == BLOCKS - 1 else ORDER):
+                engine = nc.gpsimd if (r, g) in POOL_UNITS else nc.vector
+                if lift_pd is None:
+                    pair = (joint[:], lift[:])
+                else:
+                    pair = (inv[:], lift_pd[:] if g == 0 else pd_out[:, r:r + 1])
+                for t0 in range(0, PACK, step):
+                    weight = sb.tile([P, step, P], F32, name="weight%d_%d_%d" % (r, g, t0))
+                    flat_out = weight[:].rearrange("q t m -> q (t m)")
+                    flat_in = probs[g][:, t0:t0 + step, :].rearrange("q t m -> q (t m)")
+                    if (r, g) in SCALAR_UNITS:
+                        nc.scalar.activation(out=flat_out, in_=flat_in, func=ACT.Copy, scale=joint[:])
+                        held[g] = weight
+                        continue
+                    if (r - 1, g) in SCALAR_UNITS:
+                        nc.vector.scalar_tensor_tensor(
+                            out=flat_out, in0=flat_in, scalar=joint[:],
+                            in1=held[g][:, t0:t0 + step, :].rearrange("q t m -> q (t m)"), op0=ALU.mult, op1=ALU.add,
+                        )
+                    else:
+                        engine.tensor_scalar(
+                            out=flat_out, in0=flat_in, scalar1=pair[0], scalar2=pair[1], op0=ALU.mult, op1=ALU.mult,
+                        )
+                    for t in range(t0, t0 + step):
+                        nc.tensor.matmul(
+                            out=turned[g, t // 2][:, t % 2, :], lhsT=weight[:, t - t0, :], rhs=ident[:], is_transpose=True,
+                            start=(r == 0 and t % 2 == 0), stop=(r == BLOCKS - 1 and t % 2 == 1),
+                        )
 
-        pending = None
-        for r in range(BLOCKS):
-            neg_max, prob0, sum0 = first_half(r)
-            if pending is not None:
-                weigh(*pending)
-            lift, prob1, sum1 = second_half(r, neg_max)
-            pending = (r, lift, (prob0, prob1), (sum0, sum1))
-        weigh(*pending)
+        firsts, seconds = {}, {}
+
+        def finish(r):
+            lift, lift_pd, prob1, total = seconds[r]
+            weigh(r, lift, lift_pd, (firsts[r][1], prob1), total)
+
+        for g in range(HALVES):
+            for r in range(2):
+                score(r, g)
+        for r in range(2):
+            firsts[r] = first_half(r)
+            score(2, r)
+        for r in range(2):
+            seconds[r] = second_half(r, firsts[r][0], firsts[r][2])
+            score(3, r)
+        firsts[2] = first_half(2)
+        finish(0)
+        finish(1)
+        seconds[2] = second_half(2, firsts[2][0], firsts[2][2])
+        firsts[3] = first_half(3)
+        seconds[3] = second_half(3, firsts[3][0], firsts[3][2])
+        finish(2)
+        finish(3)
 
         rounded = sb.tile([P, HALVES, X, PACK], BF16, name="rounded", align_bytes=64)
         out_rows = out_0.rearrange("(g p t) x -> g p t x", g=HALVES, t=PACK)
-        for g in (1, 0):
+        for g in ORDER[::-1]:
             result = sb.tile([P, PACK, X], F32, name="result%d" % g)
-            nc.vector.tensor_reduce(
-                out=result[:].rearrange("p t x -> p (t x)"),
-                in_=turned[g][:].rearrange("p t (x s) -> p (t x) s", s=2), axis=AXIS_X, op=ALU.add,
-            )
+            for h in range(2):
+                nc.vector.tensor_reduce(
+                    out=result[:, 2 * h:2 * h + 2, :].rearrange("p t x -> p (t x)"),
+                    in_=turned[g, h][:].rearrange("p t (x s) -> p (t x) s", s=2), axis=AXIS_X, op=ALU.add,
+                )
             nc.sync.dma_start(out=out_rows[g], in_=result[:])
-            copy = nc.scalar.copy if g == 1 else nc.vector.tensor_copy
+            copy = nc.scalar.copy if g == 0 else nc.vector.tensor_copy
             copy(
                 out=rounded[:, g].rearrange("p (c i) t -> p c t i", i=4),
                 in_=result[:].rearrange("p t (c i) -> p c t i", i=4),

@@ -18,14 +18,17 @@ ACT = mybir.ActivationFunctionType
 AXIS_X = mybir.AxisListType.X
 
 P = 128
+QUADRANT = 32
 PACK = 4
+ROWS_PER_PLACE = Q // X
 BLOCKS = Q // P
 HALVES = 2
 HALF = I // HALVES
+LIST_GROUP = 16
+SCALE_ROWS = D // 32
+SCALE_FIRST = QUADRANT - SCALE_ROWS
+SCORE_BANKS = 4
 OUT_SCALE = 512.0
-POOL_UNITS = ((0, 1), (0, 0), (1, 1))
-SCALAR_UNITS = ((2, 1),)
-ORDER = (1, 0)
 
 
 def tile_attend_ragmarginal_pl_kernel(tc, hid, voc_words, voc_scales, pd, offs, out_0, out_1, out_2):
@@ -35,57 +38,59 @@ def tile_attend_ragmarginal_pl_kernel(tc, hid, voc_words, voc_scales, pd, offs, 
         sb = ctx.enter_context(tc.tile_pool(name="sb", bufs=1))
         psum = ctx.enter_context(tc.psum_pool(name="psum", bufs=1))
 
-        offsets = lists.tile([P, I // 16], U16, name="offsets")
+        offsets = lists.tile([P, I // LIST_GROUP], U16, name="offsets")
         nc.sync.dma_start(offsets[:], offs)
 
         scale_rows = sb.tile([P, T], U8, name="scale_rows", align_bytes=64)
-        nc.sync.dma_start(out=scale_rows[16:32, :].bitcast(I32), in_=voc_scales[0].bitcast(I32))
-        for lo, hi in ((0, 16), (32, 64), (64, P)):
+        nc.sync.dma_start(out=scale_rows[SCALE_FIRST:QUADRANT, :].bitcast(I32), in_=voc_scales[0].bitcast(I32))
+        for lo, hi in ((0, SCALE_FIRST), (QUADRANT, 2 * QUADRANT), (2 * QUADRANT, P)):
             nc.vector.memset(scale_rows[lo:hi, :].bitcast(I32), 0)
 
         words = sb.tile([P, T], I32, name="words", align_bytes=64)
         nc.sync.dma_start(out=words[:], in_=voc_words[0].rearrange("p n t -> p (n t)").bitcast(I32))
+
         hid_rows = hid.rearrange("(k t) q -> k t q", t=PACK)
-        hid_half = []
-        for h in range(2):
-            part = sb.tile([P, PACK, Q // 2], F32, name="hid%d" % h)
-            nc.sync.dma_start(out=part[:], in_=hid_rows[:, :, h * (Q // 2):(h + 1) * (Q // 2)])
-            hid_half.append(part)
+        hid_parts = []
+        for part in range(2):
+            hid_part = sb.tile([P, PACK, Q // 2], F32, name="hid%d" % part)
+            nc.sync.dma_start(out=hid_part[:], in_=hid_rows[:, :, part * (Q // 2):(part + 1) * (Q // 2)])
+            hid_parts.append(hid_part)
 
-        pd_raw = sb.tile([P, 8], F32, name="pd_raw")
-        pd_rows = pd.rearrange("(x j) o -> x (j o)", j=8)
+        run = ROWS_PER_PLACE - 1
+        pd_run = sb.tile([P, ROWS_PER_PLACE], F32, name="pd_run")
+        pd_places = pd.rearrange("(x j) o -> x (j o)", j=ROWS_PER_PLACE)
         for s in range(2):
-            nc.scalar.dma_start(out=pd_raw[s:P:2, 0:7], in_=pd_rows[:, s:s + 7])
+            nc.scalar.dma_start(out=pd_run[s:P:2, 0:run], in_=pd_places[:, s:s + run])
 
-        plane = sb.tile([P, I], U8, name="plane", align_bytes=64)
-        nc.gpsimd.memset(plane[:].bitcast(I32), 0)
+        picked_plane = sb.tile([P, I], U8, name="picked_plane", align_bytes=64)
+        nc.gpsimd.memset(picked_plane[:].bitcast(I32), 0)
         ident = sb.tile([P, P], F32, name="ident")
         make_identity(nc, ident[:])
 
         pd_out = sb.tile([P, BLOCKS], F32, name="pd_out")
-        nc.scalar.activation(out=pd_out[:], in_=pd_raw[:, 0:7:2], func=ACT.Copy, scale=OUT_SCALE)
-        held = {}
+        nc.scalar.activation(out=pd_out[:], in_=pd_run[:, 0:run:2], func=ACT.Copy, scale=OUT_SCALE)
 
-        picked_scales = sb.tile([P, I], U8, name="picked_scales", align_bytes=64)
-        nc.vector.tensor_copy(picked_scales[:], scale_rows[:].indirect(offsets[:]))
-        for quad in range(4):
+        picked_rows = sb.tile([P, I], U8, name="picked_rows", align_bytes=64)
+        nc.vector.tensor_copy(picked_rows[:], scale_rows[:].indirect(offsets[:]))
+        for quad in range(P // QUADRANT):
+            first_row = SCALE_FIRST + 4 * quad
             nc.scalar.dma_start(
-                out=plane[32 * quad:32 * quad + 4, :].bitcast(I32),
-                in_=picked_scales[16 + 4 * quad:20 + 4 * quad, :].bitcast(I32),
+                out=picked_plane[QUADRANT * quad:QUADRANT * quad + 4, :].bitcast(I32),
+                in_=picked_rows[first_row:first_row + 4, :].bitcast(I32),
             )
 
-        picked = []
+        picked_words = []
         for g in range(HALVES):
-            part = sb.tile([P, HALF], U32, name="picked%d" % g, align_bytes=64)
-            cols = slice(g * (HALF // 16), (g + 1) * (HALF // 16))
-            nc.vector.tensor_copy(part[:], words[:].bitcast(U32).indirect(offsets[:, cols]))
-            picked.append(part)
+            picked = sb.tile([P, HALF], U32, name="picked%d" % g, align_bytes=64)
+            list_cols = slice(g * (HALF // LIST_GROUP), (g + 1) * (HALF // LIST_GROUP))
+            nc.vector.tensor_copy(picked[:], words[:].bitcast(U32).indirect(offsets[:, list_cols]))
+            picked_words.append(picked)
 
         dealt = {first: sb.tile([P, 2, P, PACK], BF16, name="dealt%d" % first, align_bytes=64) for first in (0, 2)}
 
-        def deal(copy, h, first):
-            src = hid_half[h][:].rearrange("k t (x r s) -> k x r t s", r=BLOCKS, s=2)
-            dst = dealt[first][:, :, h * X:(h + 1) * X, :].rearrange("k r (x s) t -> k x r t s", s=2)
+        def deal(copy, part, first):
+            src = hid_parts[part][:].rearrange("k t (x r s) -> k x r t s", r=BLOCKS, s=2)
+            dst = dealt[first][:, :, part * (P // 2):(part + 1) * (P // 2), :].rearrange("k r (x s) t -> k x r t s", s=2)
             copy(out=dst, in_=src[:, :, first:first + 2])
 
         deal(nc.scalar.copy, 0, 0)
@@ -93,167 +98,187 @@ def tile_attend_ragmarginal_pl_kernel(tc, hid, voc_words, voc_scales, pd, offs, 
         deal(nc.vector.tensor_copy, 1, 0)
         deal(nc.scalar.copy, 1, 2)
 
-        quantised = []
+        hid_mx = []
         for first, count in ((0, 1), (1, 1), (2, 2)):
             codes = sb.tile([P, count * P], U32, name="hid_codes%d" % first, align_bytes=64)
             scales = sb.tile([P, count * P], U8, name="hid_scales%d" % first, align_bytes=64)
+            in_pair = first % 2
             nc.vector.quantize_mx(
                 out=codes[:].bitcast(FP8X4), scales=scales[:],
-                in_=dealt[first - first % 2][:, first % 2:first % 2 + count, :, :].rearrange("k r p t -> k (r p t)"),
+                in_=dealt[first - in_pair][:, in_pair:in_pair + count, :, :].rearrange("k r p t -> k (r p t)"),
             )
             for j in range(count):
-                quantised.append((codes[:, j * P:(j + 1) * P], scales[:, j * P:(j + 1) * P]))
+                hid_mx.append((codes[:, j * P:(j + 1) * P], scales[:, j * P:(j + 1) * P]))
 
         scores = {}
 
         def score(r, g):
-            codes, scales = quantised[r]
-            acc = psum.tile([P, HALF], F32, name="scores%d_%d" % (r, g), tag="score_bank%d" % (len(scores) % 4))
-            nc.tensor.matmul_mx(
-                out=acc[:], lhsT=codes.bitcast(FP8X4), lhsT_scale=scales,
-                rhs=picked[g][:].bitcast(FP8X4), rhs_scale=plane[:, g * HALF:(g + 1) * HALF], start=True, stop=True,
+            codes, scales = hid_mx[r]
+            bank = psum.tile(
+                [P, HALF], F32, name="scores%d_%d" % (r, g), tag="score_bank%d" % (len(scores) % SCORE_BANKS),
             )
-            scores[r, g] = acc
+            nc.tensor.matmul_mx(
+                out=bank[:], lhsT=codes.bitcast(FP8X4), lhsT_scale=scales,
+                rhs=picked_words[g][:].bitcast(FP8X4), rhs_scale=picked_plane[:, g * HALF:(g + 1) * HALF],
+                start=True, stop=True,
+            )
+            scores[r, g] = bank
 
-        turned = {}
+        probs, sums, neg_first_max, lifts, lifted_pd, inverse = {}, {}, {}, {}, {}, {}
+
+        def exp_half(r, g, neg_shift):
+            nc.scalar.activation(
+                out=probs[r, g][:].rearrange("q (u e) m -> q u m e", e=2),
+                in_=scores[r, g][:].rearrange("q (m u e) -> q u m e", u=2, e=2),
+                func=ACT.Exp, bias=neg_shift, scale=1.0, accum_out=sums[r, g][:],
+            )
+
         negated = sb.tile([P, HALF], BF16, name="negated")
 
         def first_half(r):
-            neg_max = sb.tile([P, 1], F32, name="neg_max%d" % r)
-            prob = sb.tile([P, PACK, P], F32, name="prob%d_0" % r)
-            part_sum = sb.tile([P, 1], F32, name="part_sum%d_0" % r)
-            bank = scores[r, 0][:]
-            nc.vector.tensor_reduce(out=neg_max[:], in_=bank, axis=AXIS_X, op=ALU.max, negate=True)
-            nc.scalar.activation(
-                out=prob[:], in_=bank.rearrange("q (m t) -> q t m", t=PACK),
-                func=ACT.Exp, bias=neg_max[:], scale=1.0, accum_out=part_sum[:],
-            )
-            return neg_max, prob, part_sum
+            neg_first_max[r] = sb.tile([P, 1], F32, name="neg_first_max%d" % r)
+            probs[r, 0] = sb.tile([P, PACK, P], F32, name="prob%d_0" % r)
+            sums[r, 0] = sb.tile([P, 1], F32, name="sum%d_0" % r)
+            nc.vector.tensor_reduce(out=neg_first_max[r][:], in_=scores[r, 0][:], axis=AXIS_X, op=ALU.max, negate=True)
+            exp_half(r, 0, neg_first_max[r][:])
 
-        def second_half(r, neg_max, first_sum):
-            neg_row_max = sb.tile([P, 1], F32, name="neg_row_max%d" % r, tag="row_stat%d" % (r % 2))
-            prob = sb.tile([P, PACK, P], F32, name="prob%d_1" % r)
-            part_sum = sb.tile([P, 1], F32, name="part_sum%d_1" % r)
-            bank = scores[r, 1][:]
+        def row_slot(r):
+            return "row_slot%d" % (r % 2)
+
+        def second_half(r):
+            neg_row_max = sb.tile([P, 1], F32, name="neg_row_max%d" % r, tag=row_slot(r))
+            probs[r, 1] = sb.tile([P, PACK, P], F32, name="prob%d_1" % r)
+            sums[r, 1] = sb.tile([P, 1], F32, name="sum%d_1" % r)
             nc.vector.tensor_scalar(
-                out=negated[:], in0=bank, scalar1=-1.0, scalar2=neg_max[:], op0=ALU.mult, op1=ALU.min,
-                accum_out=neg_row_max[:],
+                out=negated[:], in0=scores[r, 1][:], scalar1=-1.0, scalar2=neg_first_max[r][:],
+                op0=ALU.mult, op1=ALU.min, accum_out=neg_row_max[:],
             )
-            lift = sb.tile([P, 1], F32, name="lift%d" % r)
-            nc.scalar.activation(out=lift[:], in_=neg_max[:], func=ACT.Exp, bias=neg_row_max[:], scale=-1.0)
+            lifts[r] = sb.tile([P, 1], F32, name="lift%d" % r)
             nc.scalar.activation(
-                out=prob[:], in_=bank.rearrange("q (m t) -> q t m", t=PACK),
-                func=ACT.Exp, bias=neg_row_max[:], scale=1.0, accum_out=part_sum[:],
+                out=lifts[r][:], in_=neg_first_max[r][:], func=ACT.Exp, bias=neg_row_max[:], scale=-1.0,
             )
-            lift_pd = None
-            if (r, 1) not in SCALAR_UNITS:
-                lift_pd = sb.tile([P, 1], F32, name="lift_pd%d" % r)
-                if (r, 0) in POOL_UNITS:
-                    nc.gpsimd.tensor_scalar(
-                        out=lift_pd[:], in0=lift[:], scalar1=pd_out[:, r:r + 1], scalar2=0.0, op0=ALU.mult, op1=ALU.add,
-                    )
-                else:
-                    nc.scalar.activation(out=lift_pd[:], in_=lift[:], func=ACT.Copy, scale=pd_out[:, r:r + 1])
-            total = sb.tile([P, 1], F32, name="total%d" % r, tag="row_stat%d" % (r % 2))
-            nc.scalar.activation(out=total[:], in_=first_sum[:], func=ACT.Identity, scale=lift[:], bias=part_sum[:])
-            return lift, lift_pd, prob, total
+            exp_half(r, 1, neg_row_max[:])
 
-        def weigh(r, lift, lift_pd, probs, total):
-            if r == 0:
-                for g in ORDER:
-                    for h in range(2):
-                        turned[g, h] = psum.tile([P, 2, P], F32, name="turned%d_%d" % (g, h), tag="result_bank%d" % len(turned))
-            inv = sb.tile([P, 1], F32, name="inv%d" % r)
-            nc.vector.reciprocal(out=inv[:], in_=total[:])
-            if (r, 1) in SCALAR_UNITS:
-                joint = sb.tile([P, 1], F32, name="joint%d" % r)
-                nc.vector.tensor_scalar(out=joint[:], in0=inv[:], scalar1=pd_out[:, r:r + 1], scalar2=None, op0=ALU.mult)
-            if (r - 1, 1) in SCALAR_UNITS:
-                joint = sb.tile([P, 1], F32, name="joint%d" % r)
-                nc.scalar.activation(out=joint[:], in_=inv[:], func=ACT.Copy, scale=pd_out[:, r:r + 1])
-            step = 2 if r == BLOCKS - 1 else PACK
-            for g in (ORDER[::-1] if r == BLOCKS - 1 else ORDER):
-                engine = nc.gpsimd if (r, g) in POOL_UNITS else nc.vector
-                if lift_pd is None:
-                    pair = (joint[:], lift[:])
-                else:
-                    pair = (inv[:], lift_pd[:] if g == 0 else pd_out[:, r:r + 1])
-                for t0 in range(0, PACK, step):
-                    weight = sb.tile([P, step, P], F32, name="weight%d_%d_%d" % (r, g, t0))
-                    flat_out = weight[:].rearrange("q t m -> q (t m)")
-                    flat_in = probs[g][:, t0:t0 + step, :].rearrange("q t m -> q (t m)")
-                    if (r, g) in SCALAR_UNITS:
-                        nc.scalar.activation(out=flat_out, in_=flat_in, func=ACT.Copy, scale=joint[:])
-                        held[g] = weight
-                        continue
-                    if (r - 1, g) in SCALAR_UNITS:
-                        nc.vector.scalar_tensor_tensor(
-                            out=flat_out, in0=flat_in, scalar=joint[:],
-                            in1=held[g][:, t0:t0 + step, :].rearrange("q t m -> q (t m)"), op0=ALU.mult, op1=ALU.add,
-                        )
-                    else:
-                        engine.tensor_scalar(
-                            out=flat_out, in0=flat_in, scalar1=pair[0], scalar2=pair[1], op0=ALU.mult, op1=ALU.mult,
-                        )
-                    for t in range(t0, t0 + step):
-                        nc.tensor.matmul(
-                            out=turned[g, t // 2][:, t % 2, :], lhsT=weight[:, t - t0, :], rhs=ident[:], is_transpose=True,
-                            start=(r == 0 and t % 2 == 0), stop=(r == BLOCKS - 1 and t % 2 == 1),
-                        )
+        def lift_pd_on_gpsimd(r):
+            lifted_pd[r] = sb.tile([P, 1], F32, name="lifted_pd%d" % r)
+            nc.gpsimd.tensor_scalar(
+                out=lifted_pd[r][:], in0=lifts[r][:], scalar1=pd_out[:, r:r + 1], scalar2=0.0,
+                op0=ALU.mult, op1=ALU.add,
+            )
 
-        firsts, seconds = {}, {}
+        def invert_row_sum(r):
+            lifted_sum = sb.tile([P, 1], F32, name="lifted_sum%d" % r)
+            row_sum = sb.tile([P, 1], F32, name="row_sum%d" % r, tag=row_slot(r))
+            nc.vector.tensor_scalar(
+                out=lifted_sum[:], in0=sums[r, 0][:], scalar1=lifts[r][:], scalar2=sums[r, 1][:],
+                op0=ALU.mult, op1=ALU.add, accum_out=row_sum[:],
+            )
+            inverse[r] = sb.tile([P, 1], F32, name="inverse%d" % r)
+            nc.vector.reciprocal(out=inverse[r][:], in_=row_sum[:])
 
-        def finish(r):
-            lift, lift_pd, prob1, total = seconds[r]
-            weigh(r, lift, lift_pd, (firsts[r][1], prob1), total)
+        turned = {}
+
+        def flat(planes):
+            return planes.rearrange("q t m -> q (t m)")
+
+        def weight_tile(r, g, t0, count):
+            return sb.tile([P, count, P], F32, name="weight%d_%d_%d" % (r, g, t0))
+
+        def turn(r, g, t0, count, weight):
+            for t in range(t0, t0 + count):
+                nc.tensor.matmul(
+                    out=turned[g, t // 2][:, t % 2, :], lhsT=weight[:, t - t0, :], rhs=ident[:], is_transpose=True,
+                    start=(r == 0 and t % 2 == 0), stop=(r == BLOCKS - 1 and t % 2 == 1),
+                )
+
+        def weigh_and_turn(engine, r, g, factor_a, factor_b, count):
+            for t0 in range(0, PACK, count):
+                weight = weight_tile(r, g, t0, count)
+                engine.tensor_scalar(
+                    out=flat(weight[:]), in0=flat(probs[r, g][:, t0:t0 + count, :]),
+                    scalar1=factor_a, scalar2=factor_b, op0=ALU.mult, op1=ALU.mult,
+                )
+                turn(r, g, t0, count, weight)
 
         for g in range(HALVES):
             for r in range(2):
                 score(r, g)
         for r in range(2):
-            firsts[r] = first_half(r)
+            first_half(r)
             score(2, r)
         for r in range(2):
-            seconds[r] = second_half(r, firsts[r][0], firsts[r][2])
+            second_half(r)
+            lift_pd_on_gpsimd(r)
             score(3, r)
-        firsts[2] = first_half(2)
-        finish(0)
-        finish(1)
-        seconds[2] = second_half(2, firsts[2][0], firsts[2][2])
-        firsts[3] = first_half(3)
-        seconds[3] = second_half(3, firsts[3][0], firsts[3][2])
-        finish(2)
-        finish(3)
+        first_half(2)
+
+        for g in (1, 0):
+            for pair in range(2):
+                turned[g, pair] = psum.tile(
+                    [P, 2, P], F32, name="turned%d_%d" % (g, pair), tag="result_bank%d" % len(turned),
+                )
+
+        invert_row_sum(0)
+        weigh_and_turn(nc.gpsimd, 0, 1, inverse[0][:], pd_out[:, 0:1], PACK)
+        weigh_and_turn(nc.gpsimd, 0, 0, inverse[0][:], lifted_pd[0][:], PACK)
+        invert_row_sum(1)
+        weigh_and_turn(nc.gpsimd, 1, 1, inverse[1][:], pd_out[:, 1:2], PACK)
+        weigh_and_turn(nc.vector, 1, 0, inverse[1][:], lifted_pd[1][:], PACK)
+
+        second_half(2)
+        first_half(3)
+        second_half(3)
+        lifted_pd[3] = sb.tile([P, 1], F32, name="lifted_pd3")
+        nc.scalar.activation(out=lifted_pd[3][:], in_=lifts[3][:], func=ACT.Copy, scale=pd_out[:, 3:4])
+
+        invert_row_sum(2)
+        joint2 = sb.tile([P, 1], F32, name="joint2")
+        nc.vector.tensor_scalar(out=joint2[:], in0=inverse[2][:], scalar1=pd_out[:, 2:3], scalar2=None, op0=ALU.mult)
+        held = weight_tile(2, 1, 0, PACK)
+        nc.scalar.activation(out=flat(held[:]), in_=flat(probs[2, 1][:]), func=ACT.Copy, scale=joint2[:])
+        weigh_and_turn(nc.vector, 2, 0, joint2[:], lifts[2][:], PACK)
+
+        invert_row_sum(3)
+        joint3 = sb.tile([P, 1], F32, name="joint3")
+        nc.scalar.activation(out=joint3[:], in_=inverse[3][:], func=ACT.Copy, scale=pd_out[:, 3:4])
+        weigh_and_turn(nc.vector, 3, 0, inverse[3][:], lifted_pd[3][:], 2)
+        for t0 in range(0, PACK, 2):
+            weight = weight_tile(3, 1, t0, 2)
+            nc.vector.scalar_tensor_tensor(
+                out=flat(weight[:]), in0=flat(probs[3, 1][:, t0:t0 + 2, :]), scalar=joint3[:],
+                in1=flat(held[:, t0:t0 + 2, :]), op0=ALU.mult, op1=ALU.add,
+            )
+            turn(3, 1, t0, 2, weight)
 
         rounded = sb.tile([P, HALVES, X, PACK], BF16, name="rounded", align_bytes=64)
-        out_rows = out_0.rearrange("(g p t) x -> g p t x", g=HALVES, t=PACK)
-        for g in ORDER[::-1]:
+        out_rows = out_0.rearrange("(g m t) x -> g m t x", g=HALVES, t=PACK)
+        for g, copy in ((0, nc.scalar.copy), (1, nc.vector.tensor_copy)):
             result = sb.tile([P, PACK, X], F32, name="result%d" % g)
-            for h in range(2):
+            for pair in range(2):
                 nc.vector.tensor_reduce(
-                    out=result[:, 2 * h:2 * h + 2, :].rearrange("p t x -> p (t x)"),
-                    in_=turned[g, h][:].rearrange("p t (x s) -> p (t x) s", s=2), axis=AXIS_X, op=ALU.add,
+                    out=result[:, 2 * pair:2 * pair + 2, :].rearrange("m t x -> m (t x)"),
+                    in_=turned[g, pair][:].rearrange("m t (x s) -> m (t x) s", s=2), axis=AXIS_X, op=ALU.add,
                 )
             nc.sync.dma_start(out=out_rows[g], in_=result[:])
-            copy = nc.scalar.copy if g == 0 else nc.vector.tensor_copy
             copy(
-                out=rounded[:, g].rearrange("p (c i) t -> p c t i", i=4),
-                in_=result[:].rearrange("p t (c i) -> p c t i", i=4),
+                out=rounded[:, g].rearrange("m (c n) t -> m c t n", n=4),
+                in_=result[:].rearrange("m t (c n) -> m c t n", n=4),
             )
 
         out_codes = sb.tile([P, HALVES * X], I32, name="out_codes", align_bytes=64)
         out_scales = sb.tile([P, HALVES * X], U8, name="out_scales", align_bytes=64)
         nc.vector.quantize_mx(
             out=out_codes[:].bitcast(FP8X4), scales=out_scales[:],
-            in_=rounded[:].rearrange("p g x t -> p (g x t)"),
+            in_=rounded[:].rearrange("m g x t -> m (g x t)"),
         )
         nc.sync.dma_start(
-            out=out_1.rearrange("g p x t -> p g (x t)").bitcast(I32),
-            in_=out_codes[:].rearrange("p (g x) -> p g x", g=HALVES),
+            out=out_1.rearrange("g m x t -> m g (x t)").bitcast(I32),
+            in_=out_codes[:].rearrange("m (g x) -> m g x", g=HALVES),
         )
-        for quad in range(4):
+        for quad in range(P // QUADRANT):
             queue = nc.scalar if quad % 2 == 0 else nc.sync
+            live_rows = out_scales[QUADRANT * quad:QUADRANT * quad + 4, :]
             queue.dma_start(
-                out=out_2[:, 4 * quad:4 * quad + 4, :].rearrange("g r x -> r g x").bitcast(I32),
-                in_=out_scales[32 * quad:32 * quad + 4, :].bitcast(I32).rearrange("r (g x) -> r g x", g=HALVES),
+                out=out_2[:, 4 * quad:4 * quad + 4, :].rearrange("g f x -> f g x").bitcast(I32),
+                in_=live_rows.bitcast(I32).rearrange("f (g x) -> f g x", g=HALVES),
             )

from contextlib import ExitStack

import concourse.mybir as mybir
from concourse.masks import make_identity

D, T, I, Q, X = 512, 4096, 1024, 512, 64
FLOPS = 2 * D * Q * I

F32 = mybir.dt.float32
BF16 = mybir.dt.bfloat16
I32 = mybir.dt.int32
U32 = mybir.dt.uint32
U16 = mybir.dt.uint16
U8 = mybir.dt.uint8
FP8X4 = mybir.dt.float8_e4m3fn_x4
ALU = mybir.AluOpType
ACT = mybir.ActivationFunctionType
AXIS_X = mybir.AxisListType.X

P = 128
QUADRANT = 32
PACK = 4
ROWS_PER_PLACE = Q // X
BLOCKS = Q // P
HALVES = 2
HALF = I // HALVES
LIST_GROUP = 16
SCALE_ROWS = D // 32
SCALE_FIRST = QUADRANT - SCALE_ROWS
SCORE_BANKS = 4
OUT_SCALE = 512.0


def tile_attend_ragmarginal_pl_kernel(tc, hid, voc_words, voc_scales, pd, offs, out_0, out_1, out_2):
    nc = tc.nc
    with ExitStack() as ctx:
        lists = ctx.enter_context(tc.tile_pool(name="lists", bufs=1))
        sb = ctx.enter_context(tc.tile_pool(name="sb", bufs=1))
        psum = ctx.enter_context(tc.psum_pool(name="psum", bufs=1))

        offsets = lists.tile([P, I // LIST_GROUP], U16, name="offsets")
        nc.sync.dma_start(offsets[:], offs)

        scale_rows = sb.tile([P, T], U8, name="scale_rows", align_bytes=64)
        nc.sync.dma_start(out=scale_rows[SCALE_FIRST:QUADRANT, :].bitcast(I32), in_=voc_scales[0].bitcast(I32))
        for lo, hi in ((0, SCALE_FIRST), (QUADRANT, 2 * QUADRANT), (2 * QUADRANT, P)):
            nc.vector.memset(scale_rows[lo:hi, :].bitcast(I32), 0)

        words = sb.tile([P, T], I32, name="words", align_bytes=64)
        nc.sync.dma_start(out=words[:], in_=voc_words[0].rearrange("p n t -> p (n t)").bitcast(I32))

        hid_rows = hid.rearrange("(k t) q -> k t q", t=PACK)
        hid_parts = []
        for part in range(2):
            hid_part = sb.tile([P, PACK, Q // 2], F32, name="hid%d" % part)
            nc.sync.dma_start(out=hid_part[:], in_=hid_rows[:, :, part * (Q // 2):(part + 1) * (Q // 2)])
            hid_parts.append(hid_part)

        run = ROWS_PER_PLACE - 1
        pd_run = sb.tile([P, ROWS_PER_PLACE], F32, name="pd_run")
        pd_places = pd.rearrange("(x j) o -> x (j o)", j=ROWS_PER_PLACE)
        for s in range(2):
            nc.scalar.dma_start(out=pd_run[s:P:2, 0:run], in_=pd_places[:, s:s + run])

        picked_plane = sb.tile([P, I], U8, name="picked_plane", align_bytes=64)
        nc.gpsimd.memset(picked_plane[:].bitcast(I32), 0)
        ident = sb.tile([P, P], F32, name="ident")
        make_identity(nc, ident[:])

        pd_out = sb.tile([P, BLOCKS], F32, name="pd_out")
        nc.scalar.activation(out=pd_out[:], in_=pd_run[:, 0:run:2], func=ACT.Copy, scale=OUT_SCALE)

        picked_rows = sb.tile([P, I], U8, name="picked_rows", align_bytes=64)
        nc.vector.tensor_copy(picked_rows[:], scale_rows[:].indirect(offsets[:]))
        for quad in range(P // QUADRANT):
            first_row = SCALE_FIRST + 4 * quad
            nc.scalar.dma_start(
                out=picked_plane[QUADRANT * quad:QUADRANT * quad + 4, :].bitcast(I32),
                in_=picked_rows[first_row:first_row + 4, :].bitcast(I32),
            )

        picked_words = []
        for g in range(HALVES):
            picked = sb.tile([P, HALF], U32, name="picked%d" % g, align_bytes=64)
            list_cols = slice(g * (HALF // LIST_GROUP), (g + 1) * (HALF // LIST_GROUP))
            nc.vector.tensor_copy(picked[:], words[:].bitcast(U32).indirect(offsets[:, list_cols]))
            picked_words.append(picked)

        dealt = {first: sb.tile([P, 2, P, PACK], BF16, name="dealt%d" % first, align_bytes=64) for first in (0, 2)}

        def deal(copy, part, first):
            src = hid_parts[part][:].rearrange("k t (x r s) -> k x r t s", r=BLOCKS, s=2)
            dst = dealt[first][:, :, part * (P // 2):(part + 1) * (P // 2), :].rearrange("k r (x s) t -> k x r t s", s=2)
            copy(out=dst, in_=src[:, :, first:first + 2])

        deal(nc.scalar.copy, 0, 0)
        deal(nc.scalar.copy, 0, 2)
        deal(nc.vector.tensor_copy, 1, 0)
        deal(nc.scalar.copy, 1, 2)

        hid_mx = []
        for first, count in ((0, 1), (1, 1), (2, 2)):
            codes = sb.tile([P, count * P], U32, name="hid_codes%d" % first, align_bytes=64)
            scales = sb.tile([P, count * P], U8, name="hid_scales%d" % first, align_bytes=64)
            in_pair = first % 2
            nc.vector.quantize_mx(
                out=codes[:].bitcast(FP8X4), scales=scales[:],
                in_=dealt[first - in_pair][:, in_pair:in_pair + count, :, :].rearrange("k r p t -> k (r p t)"),
            )
            for j in range(count):
                hid_mx.append((codes[:, j * P:(j + 1) * P], scales[:, j * P:(j + 1) * P]))

        scores = {}

        def score(r, g):
            codes, scales = hid_mx[r]
            bank = psum.tile(
                [P, HALF], F32, name="scores%d_%d" % (r, g), tag="score_bank%d" % (len(scores) % SCORE_BANKS),
            )
            nc.tensor.matmul_mx(
                out=bank[:], lhsT=codes.bitcast(FP8X4), lhsT_scale=scales,
                rhs=picked_words[g][:].bitcast(FP8X4), rhs_scale=picked_plane[:, g * HALF:(g + 1) * HALF],
                start=True, stop=True,
            )
            scores[r, g] = bank

        probs, sums, neg_first_max, lifts, lifted_pd, inverse = {}, {}, {}, {}, {}, {}

        def exp_half(r, g, neg_shift):
            nc.scalar.activation(
                out=probs[r, g][:].rearrange("q (u e) m -> q u m e", e=2),
                in_=scores[r, g][:].rearrange("q (m u e) -> q u m e", u=2, e=2),
                func=ACT.Exp, bias=neg_shift, scale=1.0, accum_out=sums[r, g][:],
            )

        negated = sb.tile([P, HALF], BF16, name="negated")

        def first_half(r):
            neg_first_max[r] = sb.tile([P, 1], F32, name="neg_first_max%d" % r)
            probs[r, 0] = sb.tile([P, PACK, P], F32, name="prob%d_0" % r)
            sums[r, 0] = sb.tile([P, 1], F32, name="sum%d_0" % r)
            nc.vector.tensor_reduce(out=neg_first_max[r][:], in_=scores[r, 0][:], axis=AXIS_X, op=ALU.max, negate=True)
            exp_half(r, 0, neg_first_max[r][:])

        def row_slot(r):
            return "row_slot%d" % (r % 2)

        def second_half(r):
            neg_row_max = sb.tile([P, 1], F32, name="neg_row_max%d" % r, tag=row_slot(r))
            probs[r, 1] = sb.tile([P, PACK, P], F32, name="prob%d_1" % r)
            sums[r, 1] = sb.tile([P, 1], F32, name="sum%d_1" % r)
            nc.vector.tensor_scalar(
                out=negated[:], in0=scores[r, 1][:], scalar1=-1.0, scalar2=neg_first_max[r][:],
                op0=ALU.mult, op1=ALU.min, accum_out=neg_row_max[:],
            )
            lifts[r] = sb.tile([P, 1], F32, name="lift%d" % r)
            nc.scalar.activation(
                out=lifts[r][:], in_=neg_first_max[r][:], func=ACT.Exp, bias=neg_row_max[:], scale=-1.0,
            )
            exp_half(r, 1, neg_row_max[:])

        def lift_pd_on_gpsimd(r):
            lifted_pd[r] = sb.tile([P, 1], F32, name="lifted_pd%d" % r)
            nc.gpsimd.tensor_scalar(
                out=lifted_pd[r][:], in0=lifts[r][:], scalar1=pd_out[:, r:r + 1], scalar2=0.0,
                op0=ALU.mult, op1=ALU.add,
            )

        def invert_row_sum(r):
            lifted_sum = sb.tile([P, 1], F32, name="lifted_sum%d" % r)
            row_sum = sb.tile([P, 1], F32, name="row_sum%d" % r, tag=row_slot(r))
            nc.vector.tensor_scalar(
                out=lifted_sum[:], in0=sums[r, 0][:], scalar1=lifts[r][:], scalar2=sums[r, 1][:],
                op0=ALU.mult, op1=ALU.add, accum_out=row_sum[:],
            )
            inverse[r] = sb.tile([P, 1], F32, name="inverse%d" % r)
            nc.vector.reciprocal(out=inverse[r][:], in_=row_sum[:])

        turned = {}

        def flat(planes):
            return planes.rearrange("q t m -> q (t m)")

        def weight_tile(r, g, t0, count):
            return sb.tile([P, count, P], F32, name="weight%d_%d_%d" % (r, g, t0))

        def turn(r, g, t0, count, weight):
            for t in range(t0, t0 + count):
                nc.tensor.matmul(
                    out=turned[g, t // 2][:, t % 2, :], lhsT=weight[:, t - t0, :], rhs=ident[:], is_transpose=True,
                    start=(r == 0 and t % 2 == 0), stop=(r == BLOCKS - 1 and t % 2 == 1),
                )

        def weigh_and_turn(engine, r, g, factor_a, factor_b, count):
            for t0 in range(0, PACK, count):
                weight = weight_tile(r, g, t0, count)
                engine.tensor_scalar(
                    out=flat(weight[:]), in0=flat(probs[r, g][:, t0:t0 + count, :]),
                    scalar1=factor_a, scalar2=factor_b, op0=ALU.mult, op1=ALU.mult,
                )
                turn(r, g, t0, count, weight)

        for g in range(HALVES):
            for r in range(2):
                score(r, g)
        for r in range(2):
            first_half(r)
            score(2, r)
        for r in range(2):
            second_half(r)
            lift_pd_on_gpsimd(r)
            score(3, r)
        first_half(2)

        for g in (1, 0):
            for pair in range(2):
                turned[g, pair] = psum.tile(
                    [P, 2, P], F32, name="turned%d_%d" % (g, pair), tag="result_bank%d" % len(turned),
                )

        invert_row_sum(0)
        weigh_and_turn(nc.gpsimd, 0, 1, inverse[0][:], pd_out[:, 0:1], PACK)
        weigh_and_turn(nc.gpsimd, 0, 0, inverse[0][:], lifted_pd[0][:], PACK)
        invert_row_sum(1)
        weigh_and_turn(nc.gpsimd, 1, 1, inverse[1][:], pd_out[:, 1:2], PACK)
        weigh_and_turn(nc.vector, 1, 0, inverse[1][:], lifted_pd[1][:], PACK)

        second_half(2)
        first_half(3)
        second_half(3)
        lifted_pd[3] = sb.tile([P, 1], F32, name="lifted_pd3")
        nc.scalar.activation(out=lifted_pd[3][:], in_=lifts[3][:], func=ACT.Copy, scale=pd_out[:, 3:4])

        invert_row_sum(2)
        joint2 = sb.tile([P, 1], F32, name="joint2")
        nc.vector.tensor_scalar(out=joint2[:], in0=inverse[2][:], scalar1=pd_out[:, 2:3], scalar2=None, op0=ALU.mult)
        held = weight_tile(2, 1, 0, PACK)
        nc.scalar.activation(out=flat(held[:]), in_=flat(probs[2, 1][:]), func=ACT.Copy, scale=joint2[:])
        weigh_and_turn(nc.vector, 2, 0, joint2[:], lifts[2][:], PACK)

        invert_row_sum(3)
        joint3 = sb.tile([P, 1], F32, name="joint3")
        nc.scalar.activation(out=joint3[:], in_=inverse[3][:], func=ACT.Copy, scale=pd_out[:, 3:4])
        weigh_and_turn(nc.vector, 3, 0, inverse[3][:], lifted_pd[3][:], 2)
        for t0 in range(0, PACK, 2):
            weight = weight_tile(3, 1, t0, 2)
            nc.vector.scalar_tensor_tensor(
                out=flat(weight[:]), in0=flat(probs[3, 1][:, t0:t0 + 2, :]), scalar=joint3[:],
                in1=flat(held[:, t0:t0 + 2, :]), op0=ALU.mult, op1=ALU.add,
            )
            turn(3, 1, t0, 2, weight)

        rounded = sb.tile([P, HALVES, X, PACK], BF16, name="rounded", align_bytes=64)
        out_rows = out_0.rearrange("(g m t) x -> g m t x", g=HALVES, t=PACK)
        for g, copy in ((0, nc.scalar.copy), (1, nc.vector.tensor_copy)):
            result = sb.tile([P, PACK, X], F32, name="result%d" % g)
            for pair in range(2):
                nc.vector.tensor_reduce(
                    out=result[:, 2 * pair:2 * pair + 2, :].rearrange("m t x -> m (t x)"),
                    in_=turned[g, pair][:].rearrange("m t (x s) -> m (t x) s", s=2), axis=AXIS_X, op=ALU.add,
                )
            nc.sync.dma_start(out=out_rows[g], in_=result[:])
            copy(
                out=rounded[:, g].rearrange("m (c n) t -> m c t n", n=4),
                in_=result[:].rearrange("m t (c n) -> m c t n", n=4),
            )

        out_codes = sb.tile([P, HALVES * X], I32, name="out_codes", align_bytes=64)
        out_scales = sb.tile([P, HALVES * X], U8, name="out_scales", align_bytes=64)
        nc.vector.quantize_mx(
            out=out_codes[:].bitcast(FP8X4), scales=out_scales[:],
            in_=rounded[:].rearrange("m g x t -> m (g x t)"),
        )
        nc.sync.dma_start(
            out=out_1.rearrange("g m x t -> m g (x t)").bitcast(I32),
            in_=out_codes[:].rearrange("m (g x) -> m g x", g=HALVES),
        )
        for quad in range(P // QUADRANT):
            queue = nc.scalar if quad % 2 == 0 else nc.sync
            live_rows = out_scales[QUADRANT * quad:QUADRANT * quad + 4, :]
            queue.dma_start(
                out=out_2[:, 4 * quad:4 * quad + 4, :].rearrange("g f x -> f g x").bitcast(I32),
                in_=live_rows.bitcast(I32).rearrange("f (g x) -> f g x", g=HALVES),
            )
